import numpy as np
import ml_dtypes


def mxq(x, axis, fmt="e4m3"):
    dtype, down = {"e4m3": (ml_dtypes.float8_e4m3fn, 7), "e5m2": (ml_dtypes.float8_e5m2, 14)}[fmt]
    v = np.moveaxis(np.asarray(x, np.float32).astype(ml_dtypes.bfloat16).astype(np.float64), axis, -1)
    blocks = v.reshape(v.shape[:-1] + (-1, 32))
    amax = np.abs(blocks).max(-1, keepdims=True)
    byte = np.maximum(np.where(amax > 0, np.frexp(amax)[1] - 1 + 127, 0) - down, 1)
    scale = np.exp2(byte - 127.0)
    codes = (blocks / scale).astype(np.float32).astype(dtype).astype(np.float64)
    return np.moveaxis((codes * scale).reshape(v.shape), -1, axis)


WIDE = False


def mx_kscale(k):
    if not WIDE:
        return np.ones(k)
    levels = np.array([10, -10, 5, -5, 0])
    if k % 512:
        return np.exp2(np.random.permutation(np.resize(levels, k // 32))).repeat(32)
    a = np.empty((k // 512, 16))
    for p in range(k // 512):
        a[p, :8] = np.random.permutation(np.resize(levels, 8))
        for g in range(8):
            far = levels[np.abs(levels - a[p, g]) >= 10]
            a[p, g + 8] = far[np.random.randint(len(far))]
    return np.exp2(a.ravel()).repeat(32)


def f64(x):
    return np.asarray(x).astype(np.float64)


def striped(idx):
    return np.tile(np.asarray(idx).reshape(-1, 16).T, (8, 1)).astype(np.uint16)


def unstriped(offs):
    return offs[:16].T.reshape(-1).astype(np.int64)


B, N, T, D, DV, NQ = 1, 1024, 2048, 512, 512, 256


def setup_inputs():
    n = np.random.standard_normal
    idx = np.random.permutation(T)[:B * N]
    s = mx_kscale(D)[:, None]
    u = np.ones(T)
    u[idx] = mx_kscale(B * N)
    r = np.random.uniform(0.5, 2.0, T)
    raw = n((D, T)) / s / (u * r)
    return {
        "qT": (n((B, D, NQ)) * s * (0.60 / np.sqrt(D))).astype(np.float32),
        "cT": raw.astype(np.float32),
        "ts": np.tile(u * r, (128, 1)).astype(np.float32),
        "kb": np.tile(n(T), (128, 1)).astype(np.float32),
        "ch": np.tile(s[:, 0] * np.random.uniform(0.5, 2.0, D), (128, 1)).astype(np.float32),
        "offs": striped(idx),
    }


def reference(qT, cT, ts, kb, ch, offs):
    idx = unstriped(offs)
    c = f64(cT)
    pick = lambda x: x[:, idx].reshape(x.shape[0], B, N).transpose(1, 0, 2)
    q = f64(qT)
    score = mxq(q, 1, "e4m3").transpose(0, 2, 1) @ mxq(pick(c), 1, "e4m3")
    score = score * pick(f64(ts))[:, :1, :]
    score = score + pick(f64(kb))[:, :1, :]
    m = score.max(-1, keepdims=True)
    p = np.exp(score - m)
    total = p.sum(-1, keepdims=True)
    w = p * pick(f64(ts))[:, :1, :]
    y = mxq(w, 2, "e4m3") @ mxq(pick(c).transpose(0, 2, 1), 1, "e4m3")
    y = y / total
    y = y * f64(ch)[:1]
    return y

@@ -1,0 +1,289 @@
+from contextlib import ExitStack
+
+import concourse.mybir as mybir
+from concourse.masks import make_identity
+
+F32 = mybir.dt.float32
+BF16 = mybir.dt.bfloat16
+U32 = mybir.dt.uint32
+U16 = mybir.dt.uint16
+U8 = mybir.dt.uint8
+FP8X4 = mybir.dt.float8_e4m3fn_x4
+ADD = mybir.AluOpType.add
+MULT = mybir.AluOpType.mult
+MAX = mybir.AluOpType.max
+X = mybir.AxisListType.X
+COPY = mybir.ActivationFunctionType.Copy
+IDENTITY = mybir.ActivationFunctionType.Identity
+EXP = mybir.ActivationFunctionType.Exp
+
+P = 128
+D = 512
+T = 2048
+N = 1024
+NQ = 256
+FLOPS = 4 * NQ * N * D
+BYTES = 4 * (D * NQ + D * N + 2 * N + D + NQ * D) + 2 * N
+
+
+def tile_attend_x_mla_bias_topk_kernel(tc, qT, cT, ts, kb, ch, offs, out):
+    nc = tc.nc
+    with ExitStack() as ctx:
+        keep = ctx.enter_context(tc.tile_pool(name="keep", bufs=1))
+        ps_s = ctx.enter_context(tc.psum_pool(name="ps_s", bufs=4))
+        ps_y = ctx.enter_context(tc.psum_pool(name="ps_y", bufs=4))
+
+        offsets = keep.tile([P, N // 16], U16, name="offsets")
+        nc.sync.dma_start(offsets[:], offs)
+
+        pool_rows = cT.rearrange("(p t) c -> p t c", t=4)
+        raws = {}
+
+        def load(u, c0, width):
+            raw = keep.tile([P, 2, width], F32, name=f"raw_{u}_{c0}")
+            nc.sync.dma_start(out=raw[:], in_=pool_rows[:, 2 * u : 2 * u + 2, c0 : c0 + width])
+            raws[(u, c0)] = raw
+
+        load(0, 0, 1024)
+        load(0, 1024, 1024)
+        ts_sb = keep.tile([P, T], F32, name="ts_sb")
+        nc.sync.dma_start(out=ts_sb[:], in_=ts)
+        kb_sb = keep.tile([P, T], F32, name="kb_sb")
+        nc.sync.dma_start(out=kb_sb[:], in_=kb)
+        load(1, 0, 1024)
+        load(1, 1024, 512)
+        load(1, 1536, 512)
+        q_raw = keep.tile([P, 4, NQ], F32, name="q_raw")
+        nc.sync.dma_start(out=q_raw[:], in_=qT[0].rearrange("(p t) q -> p t q", t=4))
+        ch_sb = keep.tile([P, D], F32, name="ch_sb")
+        nc.sync.dma_start(out=ch_sb[:], in_=ch)
+
+        ident = keep.tile([P, P], F32, name="ident")
+        make_identity(nc, ident[:])
+        warm = keep.tile([P, 1], F32, name="warm")
+        nc.vector.memset(warm[:], 0.0)
+        warmed = keep.tile([P, 1], F32, name="warmed")
+        nc.scalar.activation(warmed[:], warm[:], EXP)
+
+        def gather_row(table, name):
+            row = keep.tile([P, N], F32, name=f"{name}_row")
+            nc.vector.tensor_copy(row[:], table[:].indirect(offsets[:]))
+            return row
+
+        def columns(row, name):
+            cols = keep.tile([P, 8], F32, name=f"{name}_cols")
+            for g in range(2):
+                bank = ps_s.tile([P, 4, P], F32, name="bank_s")
+                quarters = row[:, g * 512 : (g + 1) * 512].rearrange("p (s t) -> p t s", t=4)
+                for t in range(4):
+                    nc.tensor.transpose(bank[:, t, :], quarters[:, t, :], ident[:])
+                nc.scalar.activation(cols[:, 4 * g : 4 * g + 4], bank[:, :, 0], COPY)
+            return cols
+
+        windows = [keep.tile([P, 2 * T], BF16, name=f"window{u}", align_bytes=64) for u in range(2)]
+
+        def cast(engine, u, c0, a, b):
+            dst = windows[u][:].rearrange("p (n e) -> p n e", e=2)[:, c0 + a : c0 + b, :]
+            src = raws[(u, c0)][:, :, a:b].rearrange("p e c -> p c e")
+            if engine == "scalar":
+                nc.scalar.activation(dst, src, COPY)
+            else:
+                nc.vector.tensor_copy(dst, src)
+
+        kq = keep.tile([P, N * 4], BF16, name="kq", align_bytes=64)
+
+        def gather_pairs(u, g):
+            words = kq[:].bitcast(U32).rearrange("p (g t s u) -> p g t s u", g=2, t=4, u=2)
+            dst = words[:, g, :, :, u].rearrange("p t s -> p s t")
+            nc.vector.tensor_copy(dst, windows[u][:].bitcast(U32).indirect(offsets[:, 32 * g : 32 * g + 32]))
+
+        def quantize(codes, scales, grouped):
+            nc.vector.quantize_mx(out=codes.bitcast(FP8X4), scales=scales, in_=grouped)
+
+        k_codes = keep.tile([P, N], U32, name="k_codes", align_bytes=64)
+        k_scales = keep.tile([P, N], U8, name="k_scales", align_bytes=64)
+        q_codes = keep.tile([P, NQ], U32, name="q_codes", align_bytes=64)
+        q_scales = keep.tile([P, NQ], U8, name="q_scales", align_bytes=64)
+        q_grouped = keep.tile([P, NQ * 4], BF16, name="q_grouped", align_bytes=64)
+        v_codes = keep.tile([P, 2, D], U32, name="v_codes", align_bytes=64)
+        v_scales = keep.tile([P, 2, D], U8, name="v_scales", align_bytes=64)
+        vq = keep.tile([P, 2, D * 4], BF16, name="vq", align_bytes=64)
+        y = keep.tile([P, 8, NQ], F32, name="y")
+        y_t = {}
+        pairs = kq[:].bitcast(F32).rearrange("p (g t s u) -> p g t s u", g=2, t=4, u=2)
+
+        def turn_values(g, u):
+            bank = ps_s.tile([P, 4 * P], F32, name="bank_s")
+            for t in range(4):
+                nc.tensor.transpose(bank[:, t * P : (t + 1) * P], pairs[:, g, t, :, u], ident[:])
+            nc.scalar.copy(
+                vq[:, g, :].rearrange("s (r u e t) -> s r u e t", u=2, e=2, t=4)[:, :, u],
+                bank[:].bitcast(BF16).rearrange("s (t r e) -> s r e t", t=4, e=2),
+            )
+
+        def quantize_keys(g):
+            half = slice(g * 512, (g + 1) * 512)
+            quantize(k_codes[:, half], k_scales[:, half], kq[:, g * 2048 : (g + 1) * 2048])
+
+        def quantize_values(g):
+            quantize(v_codes[:, g, :], v_scales[:, g, :], vq[:, g, :])
+
+        def scores(g):
+            banks = []
+            for half in range(2):
+                bank = ps_s.tile([P, 2, NQ], F32, name="bank_s")
+                for j in range(2):
+                    b = 4 * g + 2 * half + j
+                    cols = slice(b * P, (b + 1) * P)
+                    nc.tensor.matmul_mx(
+                        out=bank[:, j, :],
+                        lhsT=k_codes[:, cols].bitcast(FP8X4),
+                        lhsT_scale=k_scales[:, cols],
+                        rhs=q_codes[:].bitcast(FP8X4),
+                        rhs_scale=q_scales[:],
+                        start=True,
+                        stop=True,
+                    )
+                banks.append(bank)
+            return banks
+
+        def scale_scores(g, banks, engines):
+            for half in range(2):
+                for j in range(2):
+                    b = 4 * g + 2 * half + j
+                    if engines[half] == "scalar":
+                        nc.scalar.activation(
+                            y[:, b, :],
+                            banks[half][:, j, :],
+                            IDENTITY,
+                            bias=kb_cols[:, b : b + 1],
+                            scale=ts_cols[:, b : b + 1],
+                        )
+                    else:
+                        nc.vector.tensor_scalar(
+                            y[:, b, :], banks[half][:, j, :], ts_cols[:, b : b + 1], kb_cols[:, b : b + 1], MULT, ADD
+                        )
+
+        def turn_scores(g):
+            for h in range(2):
+                bank = ps_y.tile([P, 4 * P], F32, name="bank_y")
+                for t in range(4):
+                    nc.tensor.transpose(
+                        bank[:, t * P : (t + 1) * P], y[:, 4 * g + t, h * P : (h + 1) * P], ident[:]
+                    )
+                y_t[(h, g)] = bank
+
+        cast("scalar", 0, 0, 0, 1024)
+        cast("vector", 0, 1024, 0, 640)
+        cast("scalar", 0, 1024, 640, 1024)
+        gather_pairs(0, 0)
+        gather_pairs(0, 1)
+        turn_values(0, 0)
+        turn_values(1, 0)
+        ts_row = gather_row(ts_sb, "ts")
+        kb_row = gather_row(kb_sb, "kb")
+        cast("scalar", 1, 0, 0, 1024)
+        cast("vector", 1, 1024, 0, 512)
+        cast("vector", 1, 1536, 0, 320)
+        cast("scalar", 1, 1536, 320, 512)
+        ts_cols = columns(ts_row, "ts")
+        kb_cols = columns(kb_row, "kb")
+        gather_pairs(1, 0)
+        gather_pairs(1, 1)
+        turn_values(0, 1)
+        turn_values(1, 1)
+        nc.gpsimd.tensor_scalar(
+            q_grouped[:].rearrange("p (q t) -> p q t", t=4), q_raw[:].rearrange("p t q -> p q t"), 1.0, 0.0, MULT, ADD
+        )
+        quantize_keys(0)
+        quantize(q_codes[:], q_scales[:], q_grouped[:])
+        banks0 = scores(0)
+        quantize_keys(1)
+        scale_scores(0, banks0, ("scalar", "scalar"))
+        banks1 = scores(1)
+        turn_scores(0)
+        scale_scores(1, banks1, ("scalar", "vector"))
+        turn_scores(1)
+        maxima = keep.tile([P, 4], F32, name="maxima")
+        neg_max = keep.tile([P, 2], F32, name="neg_max")
+        sums = keep.tile([P, 4], F32, name="sums")
+        total = keep.tile([P, 2], F32, name="total")
+        inv = keep.tile([P, 2], F32, name="inv")
+        p = keep.tile([P, 2, N], F32, name="p")
+        for h in range(2):
+            nc.vector.reduce_max(maxima[:, 2 * h : 2 * h + 1], y_t[(h, 0)][:], axis=X)
+        for h in range(2):
+            nc.vector.reduce_max(maxima[:, 2 * h + 1 : 2 * h + 2], y_t[(h, 1)][:], axis=X)
+            nc.vector.tensor_scalar(
+                neg_max[:, h : h + 1], maxima[:, 2 * h : 2 * h + 1], maxima[:, 2 * h + 1 : 2 * h + 2], -1.0, MAX, MULT
+            )
+            for g in range(2):
+                i = 2 * h + g
+                nc.scalar.activation(
+                    p[:, h, g * 512 : (g + 1) * 512],
+                    y_t[(h, g)][:],
+                    EXP,
+                    bias=neg_max[:, h : h + 1],
+                    accum_out=sums[:, i : i + 1],
+                )
+
+        wq = keep.tile([P, 4, 512], BF16, name="wq", align_bytes=64)
+        w_codes = keep.tile([P, 4, P], U32, name="w_codes", align_bytes=64)
+        w_scales = keep.tile([P, 4, P], U8, name="w_scales", align_bytes=64)
+
+        def weights(h, g):
+            i = 2 * h + g
+            bank = ps_s.tile([P, 4, P], F32, name="bank_s")
+            for t in range(4):
+                nc.tensor.transpose(bank[:, t, :], p[:, h, g * 512 + t * P : g * 512 + (t + 1) * P], ident[:])
+            nc.vector.tensor_tensor(
+                wq[:, i, :].rearrange("s (q t) -> s q t", t=4),
+                bank[:].rearrange("s t q -> s q t"),
+                ts_cols[:, 4 * g : 4 * g + 4].unsqueeze(1).to_broadcast([P, P, 4]),
+                MULT,
+            )
+
+        def quantize_weights(h, g):
+            i = 2 * h + g
+            quantize(w_codes[:, i, :], w_scales[:, i, :], wq[:, i, :])
+
+        def product(h):
+            acc = ps_y.tile([P, D], F32, name="bank_y")
+            for g in range(2):
+                i = 2 * h + g
+                nc.tensor.matmul_mx(
+                    out=acc[:],
+                    lhsT=w_codes[:, i, :].bitcast(FP8X4),
+                    lhsT_scale=w_scales[:, i, :],
+                    rhs=v_codes[:, g, :].bitcast(FP8X4),
+                    rhs_scale=v_scales[:, g, :],
+                    start=(g == 0),
+                    stop=(g == 1),
+                )
+            return acc
+
+        def finish(h, acc, width):
+            result = keep.tile([P, D], F32, name=f"result{h}")
+            for e in range(0, D, width):
+                part = slice(e, e + width)
+                nc.vector.scalar_tensor_tensor(
+                    result[:, part], acc[:, part], inv[:, h : h + 1], ch_sb[:, part], MULT, MULT
+                )
+                nc.sync.dma_start(out=out[0, h * P : (h + 1) * P, part], in_=result[:, part])
+
+        quantize_values(0)
+        quantize_values(1)
+        weights(0, 0)
+        weights(0, 1)
+        quantize_weights(0, 0)
+        quantize_weights(0, 1)
+        nc.vector.tensor_tensor(total[:], sums[:].rearrange("p (h g) -> p g h", g=2)[:, 0, :], sums[:].rearrange("p (h g) -> p g h", g=2)[:, 1, :], ADD)
+        nc.vector.reciprocal(inv[:], total[:])
+        acc0 = product(0)
+        weights(1, 0)
+        weights(1, 1)
+        quantize_weights(1, 0)
+        quantize_weights(1, 1)
+        acc1 = product(1)
+        finish(0, acc0, D)
+        finish(1, acc1, D // 2)

@@ -30,8 +30,7 @@ def tile_attend_x_mla_bias_topk_kernel(tc, qT, cT, ts, kb, ch, offs, out):
     nc = tc.nc
     with ExitStack() as ctx:
         keep = ctx.enter_context(tc.tile_pool(name="keep", bufs=1))
-        ps_s = ctx.enter_context(tc.psum_pool(name="ps_s", bufs=4))
-        ps_y = ctx.enter_context(tc.psum_pool(name="ps_y", bufs=4))
+        psum = ctx.enter_context(tc.psum_pool(name="psum", bufs=8))
 
         offsets = keep.tile([P, N // 16], U16, name="offsets")
         nc.sync.dma_start(offsets[:], offs)
@@ -44,12 +43,12 @@ def tile_attend_x_mla_bias_topk_kernel(tc, qT, cT, ts, kb, ch, offs, out):
             nc.sync.dma_start(out=raw[:], in_=pool_rows[:, 2 * u : 2 * u + 2, c0 : c0 + width])
             raws[(u, c0)] = raw
 
-        load(0, 0, 1024)
-        load(0, 1024, 1024)
         ts_sb = keep.tile([P, T], F32, name="ts_sb")
         nc.sync.dma_start(out=ts_sb[:], in_=ts)
         kb_sb = keep.tile([P, T], F32, name="kb_sb")
         nc.sync.dma_start(out=kb_sb[:], in_=kb)
+        load(0, 0, 1024)
+        load(0, 1024, 1024)
         load(1, 0, 1024)
         load(1, 1024, 512)
         load(1, 1536, 512)
@@ -73,7 +72,7 @@ def tile_attend_x_mla_bias_topk_kernel(tc, qT, cT, ts, kb, ch, offs, out):
         def columns(row, name):
             cols = keep.tile([P, 8], F32, name=f"{name}_cols")
             for g in range(2):
-                bank = ps_s.tile([P, 4, P], F32, name="bank_s")
+                bank = psum.tile([P, 4, P], F32, name="bank")
                 quarters = row[:, g * 512 : (g + 1) * 512].rearrange("p (s t) -> p t s", t=4)
                 for t in range(4):
                     nc.tensor.transpose(bank[:, t, :], quarters[:, t, :], ident[:])
@@ -113,7 +112,7 @@ def tile_attend_x_mla_bias_topk_kernel(tc, qT, cT, ts, kb, ch, offs, out):
         pairs = kq[:].bitcast(F32).rearrange("p (g t s u) -> p g t s u", g=2, t=4, u=2)
 
         def turn_values(g, u):
-            bank = ps_s.tile([P, 4 * P], F32, name="bank_s")
+            bank = psum.tile([P, 4 * P], F32, name="bank")
             for t in range(4):
                 nc.tensor.transpose(bank[:, t * P : (t + 1) * P], pairs[:, g, t, :, u], ident[:])
             nc.scalar.copy(
@@ -128,104 +127,74 @@ def tile_attend_x_mla_bias_topk_kernel(tc, qT, cT, ts, kb, ch, offs, out):
         def quantize_values(g):
             quantize(v_codes[:, g, :], v_scales[:, g, :], vq[:, g, :])
 
-        def scores(g):
+        def scores(g, q0, width):
             banks = []
-            for half in range(2):
-                bank = ps_s.tile([P, 2, NQ], F32, name="bank_s")
+            for pair in range(2):
+                bank = psum.tile([P, 2, width], F32, name="bank")
                 for j in range(2):
-                    b = 4 * g + 2 * half + j
+                    b = 4 * g + 2 * pair + j
                     cols = slice(b * P, (b + 1) * P)
                     nc.tensor.matmul_mx(
                         out=bank[:, j, :],
                         lhsT=k_codes[:, cols].bitcast(FP8X4),
                         lhsT_scale=k_scales[:, cols],
-                        rhs=q_codes[:].bitcast(FP8X4),
-                        rhs_scale=q_scales[:],
+                        rhs=q_codes[:, q0 : q0 + width].bitcast(FP8X4),
+                        rhs_scale=q_scales[:, q0 : q0 + width],
                         start=True,
                         stop=True,
                     )
                 banks.append(bank)
             return banks
 
-        def scale_scores(g, banks, engines):
-            for half in range(2):
+        def scale_scores(g, q0, width, banks, engines):
+            for pair in range(2):
                 for j in range(2):
-                    b = 4 * g + 2 * half + j
-                    if engines[half] == "scalar":
+                    b = 4 * g + 2 * pair + j
+                    dst = y[:, b, q0 : q0 + width]
+                    if engines[pair] == "scalar":
                         nc.scalar.activation(
-                            y[:, b, :],
-                            banks[half][:, j, :],
+                            dst,
+                            banks[pair][:, j, :],
                             IDENTITY,
                             bias=kb_cols[:, b : b + 1],
                             scale=ts_cols[:, b : b + 1],
                         )
                     else:
                         nc.vector.tensor_scalar(
-                            y[:, b, :], banks[half][:, j, :], ts_cols[:, b : b + 1], kb_cols[:, b : b + 1], MULT, ADD
+                            dst, banks[pair][:, j, :], ts_cols[:, b : b + 1], kb_cols[:, b : b + 1], MULT, ADD
                         )
 
-        def turn_scores(g):
-            for h in range(2):
-                bank = ps_y.tile([P, 4 * P], F32, name="bank_y")
-                for t in range(4):
-                    nc.tensor.transpose(
-                        bank[:, t * P : (t + 1) * P], y[:, 4 * g + t, h * P : (h + 1) * P], ident[:]
-                    )
-                y_t[(h, g)] = bank
+        def turn_scores(g, h):
+            bank = psum.tile([P, 4 * P], F32, name="bank")
+            for t in range(4):
+                nc.tensor.transpose(bank[:, t * P : (t + 1) * P], y[:, 4 * g + t, h * P : (h + 1) * P], ident[:])
+            y_t[(h, g)] = bank
 
-        cast("scalar", 0, 0, 0, 1024)
-        cast("vector", 0, 1024, 0, 640)
-        cast("scalar", 0, 1024, 640, 1024)
-        gather_pairs(0, 0)
-        gather_pairs(0, 1)
-        turn_values(0, 0)
-        turn_values(1, 0)
-        ts_row = gather_row(ts_sb, "ts")
-        kb_row = gather_row(kb_sb, "kb")
-        cast("scalar", 1, 0, 0, 1024)
-        cast("vector", 1, 1024, 0, 512)
-        cast("vector", 1, 1536, 0, 320)
-        cast("scalar", 1, 1536, 320, 512)
-        ts_cols = columns(ts_row, "ts")
-        kb_cols = columns(kb_row, "kb")
-        gather_pairs(1, 0)
-        gather_pairs(1, 1)
-        turn_values(0, 1)
-        turn_values(1, 1)
-        nc.gpsimd.tensor_scalar(
-            q_grouped[:].rearrange("p (q t) -> p q t", t=4), q_raw[:].rearrange("p t q -> p q t"), 1.0, 0.0, MULT, ADD
-        )
-        quantize_keys(0)
-        quantize(q_codes[:], q_scales[:], q_grouped[:])
-        banks0 = scores(0)
-        quantize_keys(1)
-        scale_scores(0, banks0, ("scalar", "scalar"))
-        banks1 = scores(1)
-        turn_scores(0)
-        scale_scores(1, banks1, ("scalar", "vector"))
-        turn_scores(1)
         maxima = keep.tile([P, 4], F32, name="maxima")
         neg_max = keep.tile([P, 2], F32, name="neg_max")
         sums = keep.tile([P, 4], F32, name="sums")
         total = keep.tile([P, 2], F32, name="total")
         inv = keep.tile([P, 2], F32, name="inv")
         p = keep.tile([P, 2, N], F32, name="p")
-        for h in range(2):
-            nc.vector.reduce_max(maxima[:, 2 * h : 2 * h + 1], y_t[(h, 0)][:], axis=X)
-        for h in range(2):
-            nc.vector.reduce_max(maxima[:, 2 * h + 1 : 2 * h + 2], y_t[(h, 1)][:], axis=X)
+
+        def maximum(h, g):
+            i = 2 * h + g
+            nc.vector.reduce_max(maxima[:, i : i + 1], y_t[(h, g)][:], axis=X)
+
+        def negate_maximum(h):
             nc.vector.tensor_scalar(
                 neg_max[:, h : h + 1], maxima[:, 2 * h : 2 * h + 1], maxima[:, 2 * h + 1 : 2 * h + 2], -1.0, MAX, MULT
             )
-            for g in range(2):
-                i = 2 * h + g
-                nc.scalar.activation(
-                    p[:, h, g * 512 : (g + 1) * 512],
-                    y_t[(h, g)][:],
-                    EXP,
-                    bias=neg_max[:, h : h + 1],
-                    accum_out=sums[:, i : i + 1],
-                )
+
+        def exponentials(h, g):
+            i = 2 * h + g
+            nc.scalar.activation(
+                p[:, h, g * 512 : (g + 1) * 512],
+                y_t[(h, g)][:],
+                EXP,
+                bias=neg_max[:, h : h + 1],
+                accum_out=sums[:, i : i + 1],
+            )
 
         wq = keep.tile([P, 4, 512], BF16, name="wq", align_bytes=64)
         w_codes = keep.tile([P, 4, P], U32, name="w_codes", align_bytes=64)
@@ -233,7 +202,7 @@ def tile_attend_x_mla_bias_topk_kernel(tc, qT, cT, ts, kb, ch, offs, out):
 
         def weights(h, g):
             i = 2 * h + g
-            bank = ps_s.tile([P, 4, P], F32, name="bank_s")
+            bank = psum.tile([P, 4, P], F32, name="bank")
             for t in range(4):
                 nc.tensor.transpose(bank[:, t, :], p[:, h, g * 512 + t * P : g * 512 + (t + 1) * P], ident[:])
             nc.vector.tensor_tensor(
@@ -248,7 +217,7 @@ def tile_attend_x_mla_bias_topk_kernel(tc, qT, cT, ts, kb, ch, offs, out):
             quantize(w_codes[:, i, :], w_scales[:, i, :], wq[:, i, :])
 
         def product(h):
-            acc = ps_y.tile([P, D], F32, name="bank_y")
+            acc = psum.tile([P, D], F32, name="bank")
             for g in range(2):
                 i = 2 * h + g
                 nc.tensor.matmul_mx(
@@ -271,19 +240,68 @@ def tile_attend_x_mla_bias_topk_kernel(tc, qT, cT, ts, kb, ch, offs, out):
                 )
                 nc.sync.dma_start(out=out[0, h * P : (h + 1) * P, part], in_=result[:, part])
 
+        def divide(h):
+            nc.vector.tensor_tensor(
+                total[:, h : h + 1], sums[:, 2 * h : 2 * h + 1], sums[:, 2 * h + 1 : 2 * h + 2], ADD
+            )
+            nc.vector.reciprocal(inv[:, h : h + 1], total[:, h : h + 1])
+
+        ts_row = gather_row(ts_sb, "ts")
+        kb_row = gather_row(kb_sb, "kb")
+        cast("vector", 0, 0, 0, 1024)
+        cast("vector", 0, 1024, 0, 1024)
+        cast("scalar", 1, 0, 0, 1024)
+        gather_pairs(0, 0)
+        gather_pairs(0, 1)
+        cast("vector", 1, 1024, 0, 512)
+        cast("vector", 1, 1536, 0, 512)
+        ts_cols = columns(ts_row, "ts")
+        gather_pairs(1, 0)
+        gather_pairs(1, 1)
+        quantize_keys(0)
+        nc.gpsimd.tensor_scalar(
+            q_grouped[:].rearrange("p (q t) -> p q t", t=4), q_raw[:].rearrange("p t q -> p q t"), 1.0, 0.0, MULT, ADD
+        )
+        quantize(q_codes[:], q_scales[:], q_grouped[:])
+        quantize_keys(1)
+        kb_cols = columns(kb_row, "kb")
+
+        engines = ("vector", "scalar")
+        banks00 = scores(0, 0, P)
+        banks1 = scores(1, 0, NQ)
+        scale_scores(1, 0, NQ, banks1, engines)
+        scale_scores(0, 0, P, banks00, engines)
+        turn_scores(1, 0)
+        maximum(0, 1)
+        turn_scores(0, 0)
+        banks01 = scores(0, P, P)
+        maximum(0, 0)
+        negate_maximum(0)
+        scale_scores(0, P, P, banks01, engines)
+        turn_scores(1, 1)
+        turn_scores(0, 1)
+        for g in range(2):
+            for u in range(2):
+                turn_values(g, u)
+        maximum(1, 0)
+        maximum(1, 1)
+        negate_maximum(1)
+        for h in range(2):
+            for g in range(2):
+                exponentials(h, g)
         quantize_values(0)
         quantize_values(1)
         weights(0, 0)
         weights(0, 1)
         quantize_weights(0, 0)
-        quantize_weights(0, 1)
-        nc.vector.tensor_tensor(total[:], sums[:].rearrange("p (h g) -> p g h", g=2)[:, 0, :], sums[:].rearrange("p (h g) -> p g h", g=2)[:, 1, :], ADD)
-        nc.vector.reciprocal(inv[:], total[:])
-        acc0 = product(0)
         weights(1, 0)
-        weights(1, 1)
+        quantize_weights(0, 1)
+        acc0 = product(0)
         quantize_weights(1, 0)
+        weights(1, 1)
         quantize_weights(1, 1)
+        divide(0)
+        divide(1)
         acc1 = product(1)
         finish(0, acc0, D)
         finish(1, acc1, D // 2)

@@ -43,17 +43,20 @@ def tile_attend_x_mla_bias_topk_kernel(tc, qT, cT, ts, kb, ch, offs, out):
             nc.sync.dma_start(out=raw[:], in_=pool_rows[:, 2 * u : 2 * u + 2, c0 : c0 + width])
             raws[(u, c0)] = raw
 
-        ts_sb = keep.tile([P, T], F32, name="ts_sb")
-        nc.sync.dma_start(out=ts_sb[:], in_=ts)
-        kb_sb = keep.tile([P, T], F32, name="kb_sb")
-        nc.sync.dma_start(out=kb_sb[:], in_=kb)
+        def load_table(table, name):
+            tile = keep.tile([P, T], F32, name=f"{name}_table")
+            nc.sync.dma_start(out=tile[:], in_=table)
+            return tile
+
+        kb_sb = load_table(kb, "kb")
         load(0, 0, 1024)
         load(0, 1024, 1024)
+        ts_sb = load_table(ts, "ts")
         load(1, 0, 1024)
-        load(1, 1024, 512)
-        load(1, 1536, 512)
         q_raw = keep.tile([P, 4, NQ], F32, name="q_raw")
         nc.sync.dma_start(out=q_raw[:], in_=qT[0].rearrange("(p t) q -> p t q", t=4))
+        load(1, 1024, 512)
+        load(1, 1536, 512)
         ch_sb = keep.tile([P, D], F32, name="ch_sb")
         nc.sync.dma_start(out=ch_sb[:], in_=ch)
 
@@ -127,42 +130,34 @@ def tile_attend_x_mla_bias_topk_kernel(tc, qT, cT, ts, kb, ch, offs, out):
         def quantize_values(g):
             quantize(v_codes[:, g, :], v_scales[:, g, :], vq[:, g, :])
 
-        def scores(g, q0, width):
-            banks = []
-            for pair in range(2):
-                bank = psum.tile([P, 2, width], F32, name="bank")
-                for j in range(2):
-                    b = 4 * g + 2 * pair + j
-                    cols = slice(b * P, (b + 1) * P)
-                    nc.tensor.matmul_mx(
-                        out=bank[:, j, :],
-                        lhsT=k_codes[:, cols].bitcast(FP8X4),
-                        lhsT_scale=k_scales[:, cols],
-                        rhs=q_codes[:, q0 : q0 + width].bitcast(FP8X4),
-                        rhs_scale=q_scales[:, q0 : q0 + width],
-                        start=True,
-                        stop=True,
-                    )
-                banks.append(bank)
-            return banks
+        def scores(g, h):
+            bank = psum.tile([P, 4, P], F32, name="bank")
+            queries = slice(h * P, (h + 1) * P)
+            for t in range(4):
+                cols = slice((4 * g + t) * P, (4 * g + t + 1) * P)
+                nc.tensor.matmul_mx(
+                    out=bank[:, t, :],
+                    lhsT=k_codes[:, cols].bitcast(FP8X4),
+                    lhsT_scale=k_scales[:, cols],
+                    rhs=q_codes[:, queries].bitcast(FP8X4),
+                    rhs_scale=q_scales[:, queries],
+                    start=True,
+                    stop=True,
+                )
+            return bank
 
-        def scale_scores(g, q0, width, banks, engines):
-            for pair in range(2):
-                for j in range(2):
-                    b = 4 * g + 2 * pair + j
-                    dst = y[:, b, q0 : q0 + width]
-                    if engines[pair] == "scalar":
-                        nc.scalar.activation(
-                            dst,
-                            banks[pair][:, j, :],
-                            IDENTITY,
-                            bias=kb_cols[:, b : b + 1],
-                            scale=ts_cols[:, b : b + 1],
-                        )
-                    else:
-                        nc.vector.tensor_scalar(
-                            dst, banks[pair][:, j, :], ts_cols[:, b : b + 1], kb_cols[:, b : b + 1], MULT, ADD
-                        )
+        def scale_scores(g, h, bank):
+            for t in range(4):
+                b = 4 * g + t
+                dst = y[:, b, h * P : (h + 1) * P]
+                if g == 1:
+                    nc.scalar.activation(
+                        dst, bank[:, t, :], IDENTITY, bias=kb_cols[:, b : b + 1], scale=ts_cols[:, b : b + 1]
+                    )
+                else:
+                    nc.vector.tensor_scalar(
+                        dst, bank[:, t, :], ts_cols[:, b : b + 1], kb_cols[:, b : b + 1], MULT, ADD
+                    )
 
         def turn_scores(g, h):
             bank = psum.tile([P, 4 * P], F32, name="bank")
@@ -246,43 +241,46 @@ def tile_attend_x_mla_bias_topk_kernel(tc, qT, cT, ts, kb, ch, offs, out):
             )
             nc.vector.reciprocal(inv[:, h : h + 1], total[:, h : h + 1])
 
-        ts_row = gather_row(ts_sb, "ts")
         kb_row = gather_row(kb_sb, "kb")
-        cast("vector", 0, 0, 0, 1024)
+        cast("scalar", 0, 0, 0, 1024)
         cast("vector", 0, 1024, 0, 1024)
+        ts_row = gather_row(ts_sb, "ts")
         cast("scalar", 1, 0, 0, 1024)
         gather_pairs(0, 0)
         gather_pairs(0, 1)
-        cast("vector", 1, 1024, 0, 512)
-        cast("vector", 1, 1536, 0, 512)
-        ts_cols = columns(ts_row, "ts")
-        gather_pairs(1, 0)
-        gather_pairs(1, 1)
-        quantize_keys(0)
         nc.gpsimd.tensor_scalar(
             q_grouped[:].rearrange("p (q t) -> p q t", t=4), q_raw[:].rearrange("p t q -> p q t"), 1.0, 0.0, MULT, ADD
         )
         quantize(q_codes[:], q_scales[:], q_grouped[:])
+        cast("scalar", 1, 1024, 0, 512)
+        cast("vector", 1, 1536, 0, 384)
+        cast("scalar", 1, 1536, 384, 512)
+        turn_values(0, 0)
+        turn_values(1, 0)
+        gather_pairs(1, 0)
+        gather_pairs(1, 1)
+        quantize_keys(0)
         quantize_keys(1)
         kb_cols = columns(kb_row, "kb")
+        ts_cols = columns(ts_row, "ts")
 
-        engines = ("vector", "scalar")
-        banks00 = scores(0, 0, P)
-        banks1 = scores(1, 0, NQ)
-        scale_scores(1, 0, NQ, banks1, engines)
-        scale_scores(0, 0, P, banks00, engines)
-        turn_scores(1, 0)
-        maximum(0, 1)
+        bank00 = scores(0, 0)
+        bank10 = scores(1, 0)
+        scale_scores(0, 0, bank00)
+        scale_scores(1, 0, bank10)
         turn_scores(0, 0)
-        banks01 = scores(0, P, P)
+        bank01 = scores(0, 1)
+        bank11 = scores(1, 1)
+        scale_scores(0, 1, bank01)
         maximum(0, 0)
+        turn_scores(1, 0)
+        scale_scores(1, 1, bank11)
+        maximum(0, 1)
         negate_maximum(0)
-        scale_scores(0, P, P, banks01, engines)
-        turn_scores(1, 1)
         turn_scores(0, 1)
-        for g in range(2):
-            for u in range(2):
-                turn_values(g, u)
+        turn_scores(1, 1)
+        turn_values(0, 1)
+        turn_values(1, 1)
         maximum(1, 0)
         maximum(1, 1)
         negate_maximum(1)

@@ -30,7 +30,8 @@ def tile_attend_x_mla_bias_topk_kernel(tc, qT, cT, ts, kb, ch, offs, out):
     nc = tc.nc
     with ExitStack() as ctx:
         keep = ctx.enter_context(tc.tile_pool(name="keep", bufs=1))
-        psum = ctx.enter_context(tc.psum_pool(name="psum", bufs=8))
+        psum_s = ctx.enter_context(tc.psum_pool(name="psum_s", bufs=4))
+        psum_y = ctx.enter_context(tc.psum_pool(name="psum_y", bufs=4))
 
         offsets = keep.tile([P, N // 16], U16, name="offsets")
         nc.sync.dma_start(offsets[:], offs)
@@ -49,14 +50,14 @@ def tile_attend_x_mla_bias_topk_kernel(tc, qT, cT, ts, kb, ch, offs, out):
             return tile
 
         kb_sb = load_table(kb, "kb")
-        load(0, 0, 1024)
-        load(0, 1024, 1024)
         ts_sb = load_table(ts, "ts")
+        load(0, 1024, 1024)
+        load(0, 0, 1024)
+        load(1, 1536, 512)
+        load(1, 1024, 512)
         load(1, 0, 1024)
         q_raw = keep.tile([P, 4, NQ], F32, name="q_raw")
         nc.sync.dma_start(out=q_raw[:], in_=qT[0].rearrange("(p t) q -> p t q", t=4))
-        load(1, 1024, 512)
-        load(1, 1536, 512)
         ch_sb = keep.tile([P, D], F32, name="ch_sb")
         nc.sync.dma_start(out=ch_sb[:], in_=ch)
 
@@ -72,15 +73,15 @@ def tile_attend_x_mla_bias_topk_kernel(tc, qT, cT, ts, kb, ch, offs, out):
             nc.vector.tensor_copy(row[:], table[:].indirect(offsets[:]))
             return row
 
-        def columns(row, name):
-            cols = keep.tile([P, 8], F32, name=f"{name}_cols")
-            for g in range(2):
-                bank = psum.tile([P, 4, P], F32, name="bank")
-                quarters = row[:, g * 512 : (g + 1) * 512].rearrange("p (s t) -> p t s", t=4)
-                for t in range(4):
-                    nc.tensor.transpose(bank[:, t, :], quarters[:, t, :], ident[:])
-                nc.scalar.activation(cols[:, 4 * g : 4 * g + 4], bank[:, :, 0], COPY)
-            return cols
+        ts_cols = keep.tile([P, 8], F32, name="ts_cols")
+        kb_cols = keep.tile([P, 8], F32, name="kb_cols")
+
+        def columns(row, cols, pool, g):
+            bank = pool.tile([P, 4, P], F32, name="bank")
+            quarters = row[:, g * 512 : (g + 1) * 512].rearrange("p (s t) -> p t s", t=4)
+            for t in range(4):
+                nc.tensor.transpose(bank[:, t, :], quarters[:, t, :], ident[:])
+            nc.scalar.activation(cols[:, 4 * g : 4 * g + 4], bank[:, :, 0], COPY)
 
         windows = [keep.tile([P, 2 * T], BF16, name=f"window{u}", align_bytes=64) for u in range(2)]
 
@@ -114,11 +115,11 @@ def tile_attend_x_mla_bias_topk_kernel(tc, qT, cT, ts, kb, ch, offs, out):
         y_t = {}
         pairs = kq[:].bitcast(F32).rearrange("p (g t s u) -> p g t s u", g=2, t=4, u=2)
 
-        def turn_values(g, u):
-            bank = psum.tile([P, 4 * P], F32, name="bank")
+        def turn_values(g, u, copy):
+            bank = psum_y.tile([P, 4 * P], F32, name="bank")
             for t in range(4):
                 nc.tensor.transpose(bank[:, t * P : (t + 1) * P], pairs[:, g, t, :, u], ident[:])
-            nc.scalar.copy(
+            copy(
                 vq[:, g, :].rearrange("s (r u e t) -> s r u e t", u=2, e=2, t=4)[:, :, u],
                 bank[:].bitcast(BF16).rearrange("s (t r e) -> s r e t", t=4, e=2),
             )
@@ -131,7 +132,7 @@ def tile_attend_x_mla_bias_topk_kernel(tc, qT, cT, ts, kb, ch, offs, out):
             quantize(v_codes[:, g, :], v_scales[:, g, :], vq[:, g, :])
 
         def scores(g, h):
-            bank = psum.tile([P, 4, P], F32, name="bank")
+            bank = psum_y.tile([P, 4, P], F32, name="bank")
             queries = slice(h * P, (h + 1) * P)
             for t in range(4):
                 cols = slice((4 * g + t) * P, (4 * g + t + 1) * P)
@@ -146,11 +147,11 @@ def tile_attend_x_mla_bias_topk_kernel(tc, qT, cT, ts, kb, ch, offs, out):
                 )
             return bank
 
-        def scale_scores(g, h, bank):
+        def scale_scores(g, h, bank, engine):
             for t in range(4):
                 b = 4 * g + t
                 dst = y[:, b, h * P : (h + 1) * P]
-                if g == 1:
+                if engine == "scalar":
                     nc.scalar.activation(
                         dst, bank[:, t, :], IDENTITY, bias=kb_cols[:, b : b + 1], scale=ts_cols[:, b : b + 1]
                     )
@@ -160,7 +161,7 @@ def tile_attend_x_mla_bias_topk_kernel(tc, qT, cT, ts, kb, ch, offs, out):
                     )
 
         def turn_scores(g, h):
-            bank = psum.tile([P, 4 * P], F32, name="bank")
+            bank = psum_y.tile([P, 4 * P], F32, name="bank")
             for t in range(4):
                 nc.tensor.transpose(bank[:, t * P : (t + 1) * P], y[:, 4 * g + t, h * P : (h + 1) * P], ident[:])
             y_t[(h, g)] = bank
@@ -195,14 +196,19 @@ def tile_attend_x_mla_bias_topk_kernel(tc, qT, cT, ts, kb, ch, offs, out):
         w_codes = keep.tile([P, 4, P], U32, name="w_codes", align_bytes=64)
         w_scales = keep.tile([P, 4, P], U8, name="w_scales", align_bytes=64)
 
-        def weights(h, g):
-            i = 2 * h + g
-            bank = psum.tile([P, 4, P], F32, name="bank")
+        p_t = {}
+
+        def turn_exponentials(h, g):
+            bank = psum_y.tile([P, 4, P], F32, name="bank")
             for t in range(4):
                 nc.tensor.transpose(bank[:, t, :], p[:, h, g * 512 + t * P : g * 512 + (t + 1) * P], ident[:])
+            p_t[(h, g)] = bank
+
+        def weights(h, g):
+            i = 2 * h + g
             nc.vector.tensor_tensor(
                 wq[:, i, :].rearrange("s (q t) -> s q t", t=4),
-                bank[:].rearrange("s t q -> s q t"),
+                p_t[(h, g)][:].rearrange("s t q -> s q t"),
                 ts_cols[:, 4 * g : 4 * g + 4].unsqueeze(1).to_broadcast([P, P, 4]),
                 MULT,
             )
@@ -212,7 +218,7 @@ def tile_attend_x_mla_bias_topk_kernel(tc, qT, cT, ts, kb, ch, offs, out):
             quantize(w_codes[:, i, :], w_scales[:, i, :], wq[:, i, :])
 
         def product(h):
-            acc = psum.tile([P, D], F32, name="bank")
+            acc = psum_s.tile([P, D], F32, name="bank")
             for g in range(2):
                 i = 2 * h + g
                 nc.tensor.matmul_mx(
@@ -241,65 +247,71 @@ def tile_attend_x_mla_bias_topk_kernel(tc, qT, cT, ts, kb, ch, offs, out):
             )
             nc.vector.reciprocal(inv[:, h : h + 1], total[:, h : h + 1])
 
-        kb_row = gather_row(kb_sb, "kb")
-        cast("scalar", 0, 0, 0, 1024)
-        cast("vector", 0, 1024, 0, 1024)
-        ts_row = gather_row(ts_sb, "ts")
-        cast("scalar", 1, 0, 0, 1024)
-        gather_pairs(0, 0)
-        gather_pairs(0, 1)
-        nc.gpsimd.tensor_scalar(
-            q_grouped[:].rearrange("p (q t) -> p q t", t=4), q_raw[:].rearrange("p t q -> p q t"), 1.0, 0.0, MULT, ADD
-        )
-        quantize(q_codes[:], q_scales[:], q_grouped[:])
+        banks = {}
+        accs = {}
         cast("scalar", 1, 1024, 0, 512)
-        cast("vector", 1, 1536, 0, 384)
-        cast("scalar", 1, 1536, 384, 512)
-        turn_values(0, 0)
-        turn_values(1, 0)
+        cast("vector", 1, 0, 0, 1024)
+        cast("vector", 0, 0, 0, 1024)
+        cast("vector", 0, 1024, 0, 1024)
+        gather_pairs(0, 1)
+        kb_row = gather_row(kb_sb, "kb")
+        cast("vector", 1, 1536, 0, 128)
+        cast("scalar", 1, 1536, 128, 512)
+        nc.scalar.activation(q_grouped[:].rearrange("p (q t) -> p q t", t=4), q_raw[:].rearrange("p t q -> p q t"), COPY)
         gather_pairs(1, 0)
+        columns(kb_row, kb_cols, psum_s, 1)
+        gather_pairs(0, 0)
         gather_pairs(1, 1)
         quantize_keys(0)
+        ts_row = gather_row(ts_sb, "ts")
+        columns(ts_row, ts_cols, psum_s, 1)
+        quantize(q_codes[:], q_scales[:], q_grouped[:])
+        turn_values(0, 1, nc.scalar.copy)
         quantize_keys(1)
-        kb_cols = columns(kb_row, "kb")
-        ts_cols = columns(ts_row, "ts")
-
-        bank00 = scores(0, 0)
-        bank10 = scores(1, 0)
-        scale_scores(0, 0, bank00)
-        scale_scores(1, 0, bank10)
-        turn_scores(0, 0)
-        bank01 = scores(0, 1)
-        bank11 = scores(1, 1)
-        scale_scores(0, 1, bank01)
-        maximum(0, 0)
-        turn_scores(1, 0)
-        scale_scores(1, 1, bank11)
-        maximum(0, 1)
-        negate_maximum(0)
-        turn_scores(0, 1)
-        turn_scores(1, 1)
-        turn_values(0, 1)
-        turn_values(1, 1)
-        maximum(1, 0)
-        maximum(1, 1)
-        negate_maximum(1)
-        for h in range(2):
-            for g in range(2):
-                exponentials(h, g)
+        banks[(0, 0)] = scores(0, 0)
+        turn_values(0, 0, nc.scalar.copy)
+        columns(ts_row, ts_cols, psum_s, 0)
+        columns(kb_row, kb_cols, psum_s, 0)
+        banks[(1, 0)] = scores(1, 0)
+        banks[(1, 1)] = scores(1, 1)
+        turn_values(1, 0, nc.scalar.copy)
+        turn_values(1, 1, nc.vector.tensor_copy)
         quantize_values(0)
+        banks[(0, 1)] = scores(0, 1)
+        scale_scores(0, 0, banks[(0, 0)], "scalar")
+        scale_scores(1, 0, banks[(1, 0)], "scalar")
+        turn_scores(1, 0)
+        maximum(0, 1)
+        scale_scores(0, 1, banks[(0, 1)], "scalar")
         quantize_values(1)
-        weights(0, 0)
-        weights(0, 1)
-        quantize_weights(0, 0)
+        turn_scores(0, 0)
+        maximum(0, 0)
+        scale_scores(1, 1, banks[(1, 1)], "scalar")
+        turn_scores(0, 1)
+        negate_maximum(0)
+        turn_scores(1, 1)
+        exponentials(0, 0)
+        maximum(1, 1)
+        turn_exponentials(0, 0)
+        maximum(1, 0)
+        negate_maximum(1)
+        exponentials(1, 0)
+        exponentials(1, 1)
+        turn_exponentials(1, 0)
+        exponentials(0, 1)
+        turn_exponentials(0, 1)
+        divide(0)
+        turn_exponentials(1, 1)
         weights(1, 0)
-        quantize_weights(0, 1)
-        acc0 = product(0)
+        weights(0, 0)
+        quantize_weights(0, 0)
+        weights(0, 1)
         quantize_weights(1, 0)
+        quantize_weights(0, 1)
         weights(1, 1)
         quantize_weights(1, 1)
-        divide(0)
         divide(1)
-        acc1 = product(1)
-        finish(0, acc0, D)
-        finish(1, acc1, D // 2)
+        accs[0] = product(0)
+        finish(0, accs[0], D // 1)
+        accs[1] = product(1)
+        finish(1, accs[1], D // 2)

@@ -22,7 +22,10 @@ D = 512
 T = 2048
 N = 1024
 NQ = 256
-FLOPS = 4 * NQ * N * D
+HALF = N // 2
+PLACES = 4
+
+FLOPS = 2 * (2 * NQ * N * D)
 BYTES = 4 * (D * NQ + D * N + 2 * N + D + NQ * D) + 2 * N
 
 
@@ -30,288 +33,298 @@ def tile_attend_x_mla_bias_topk_kernel(tc, qT, cT, ts, kb, ch, offs, out):
     nc = tc.nc
     with ExitStack() as ctx:
         keep = ctx.enter_context(tc.tile_pool(name="keep", bufs=1))
-        psum_s = ctx.enter_context(tc.psum_pool(name="psum_s", bufs=4))
-        psum_y = ctx.enter_context(tc.psum_pool(name="psum_y", bufs=4))
+        score_banks = ctx.enter_context(tc.psum_pool(name="score_banks", bufs=3))
+        other_banks = ctx.enter_context(tc.psum_pool(name="other_banks", bufs=5))
 
         offsets = keep.tile([P, N // 16], U16, name="offsets")
         nc.sync.dma_start(offsets[:], offs)
 
-        pool_rows = cT.rearrange("(p t) c -> p t c", t=4)
-        raws = {}
+        latent_rows = cT.rearrange("(p f) c -> p f c", f=PLACES)
+        chunks = {}
 
-        def load(u, c0, width):
-            raw = keep.tile([P, 2, width], F32, name=f"raw_{u}_{c0}")
-            nc.sync.dma_start(out=raw[:], in_=pool_rows[:, 2 * u : 2 * u + 2, c0 : c0 + width])
-            raws[(u, c0)] = raw
+        def load_chunk(u, first, width):
+            chunk = keep.tile([P, 2, width], F32, name=f"chunk_{u}_{first}")
+            nc.sync.dma_start(
+                out=chunk[:], in_=latent_rows[:, 2 * u : 2 * u + 2, first : first + width]
+            )
+            chunks[(u, first)] = chunk
 
         def load_table(table, name):
             tile = keep.tile([P, T], F32, name=f"{name}_table")
             nc.sync.dma_start(out=tile[:], in_=table)
             return tile
 
-        kb_sb = load_table(kb, "kb")
-        ts_sb = load_table(ts, "ts")
-        load(0, 1024, 1024)
-        load(0, 0, 1024)
-        load(1, 1536, 512)
-        load(1, 1024, 512)
-        load(1, 0, 1024)
-        q_raw = keep.tile([P, 4, NQ], F32, name="q_raw")
-        nc.sync.dma_start(out=q_raw[:], in_=qT[0].rearrange("(p t) q -> p t q", t=4))
-        ch_sb = keep.tile([P, D], F32, name="ch_sb")
-        nc.sync.dma_start(out=ch_sb[:], in_=ch)
+        load_chunk(0, 0, 1024)
+        load_chunk(0, 1024, 1024)
+        load_chunk(1, 1536, 512)
+        kb_table = load_table(kb, "kb")
+        ts_table = load_table(ts, "ts")
+        load_chunk(1, 1024, 512)
+        load_chunk(1, 0, 1024)
+        q_raw = keep.tile([P, PLACES, NQ], F32, name="q_raw")
+        nc.sync.dma_start(out=q_raw[:], in_=qT[0].rearrange("(p f) q -> p f q", f=PLACES))
+        ch_tile = keep.tile([P, D], F32, name="ch_tile")
+        nc.sync.dma_start(out=ch_tile[:], in_=ch)
 
-        ident = keep.tile([P, P], F32, name="ident")
-        make_identity(nc, ident[:])
-        warm = keep.tile([P, 1], F32, name="warm")
-        nc.vector.memset(warm[:], 0.0)
-        warmed = keep.tile([P, 1], F32, name="warmed")
-        nc.scalar.activation(warmed[:], warm[:], EXP)
-
-        def gather_row(table, name):
-            row = keep.tile([P, N], F32, name=f"{name}_row")
-            nc.vector.tensor_copy(row[:], table[:].indirect(offsets[:]))
-            return row
-
-        ts_cols = keep.tile([P, 8], F32, name="ts_cols")
-        kb_cols = keep.tile([P, 8], F32, name="kb_cols")
-
-        def columns(row, cols, pool, g):
-            bank = pool.tile([P, 4, P], F32, name="bank")
-            quarters = row[:, g * 512 : (g + 1) * 512].rearrange("p (s t) -> p t s", t=4)
-            for t in range(4):
-                nc.tensor.transpose(bank[:, t, :], quarters[:, t, :], ident[:])
-            nc.scalar.activation(cols[:, 4 * g : 4 * g + 4], bank[:, :, 0], COPY)
+        identity = keep.tile([P, P], F32, name="identity")
+        make_identity(nc, identity[:])
+        zero = keep.tile([P, 1], F32, name="zero")
+        nc.vector.memset(zero[:], 0.0)
+        one = keep.tile([P, 1], F32, name="one")
+        nc.scalar.activation(one[:], zero[:], EXP)
 
         windows = [keep.tile([P, 2 * T], BF16, name=f"window{u}", align_bytes=64) for u in range(2)]
+        grouped = keep.tile([P, N * PLACES], BF16, name="grouped", align_bytes=64)
+        kb_row = keep.tile([P, N], F32, name="kb_row")
+        ts_row = keep.tile([P, N], F32, name="ts_row")
 
-        def cast(engine, u, c0, a, b):
-            dst = windows[u][:].rearrange("p (n e) -> p n e", e=2)[:, c0 + a : c0 + b, :]
-            src = raws[(u, c0)][:, :, a:b].rearrange("p e c -> p c e")
-            if engine == "scalar":
-                nc.scalar.activation(dst, src, COPY)
-            else:
-                nc.vector.tensor_copy(dst, src)
-
-        kq = keep.tile([P, N * 4], BF16, name="kq", align_bytes=64)
-
-        def gather_pairs(u, g):
-            words = kq[:].bitcast(U32).rearrange("p (g t s u) -> p g t s u", g=2, t=4, u=2)
-            dst = words[:, g, :, :, u].rearrange("p t s -> p s t")
-            nc.vector.tensor_copy(dst, windows[u][:].bitcast(U32).indirect(offsets[:, 32 * g : 32 * g + 32]))
-
-        def quantize(codes, scales, grouped):
-            nc.vector.quantize_mx(out=codes.bitcast(FP8X4), scales=scales, in_=grouped)
-
-        k_codes = keep.tile([P, N], U32, name="k_codes", align_bytes=64)
-        k_scales = keep.tile([P, N], U8, name="k_scales", align_bytes=64)
-        q_codes = keep.tile([P, NQ], U32, name="q_codes", align_bytes=64)
-        q_scales = keep.tile([P, NQ], U8, name="q_scales", align_bytes=64)
-        q_grouped = keep.tile([P, NQ * 4], BF16, name="q_grouped", align_bytes=64)
-        v_codes = keep.tile([P, 2, D], U32, name="v_codes", align_bytes=64)
-        v_scales = keep.tile([P, 2, D], U8, name="v_scales", align_bytes=64)
-        vq = keep.tile([P, 2, D * 4], BF16, name="vq", align_bytes=64)
-        y = keep.tile([P, 8, NQ], F32, name="y")
-        y_t = {}
-        pairs = kq[:].bitcast(F32).rearrange("p (g t s u) -> p g t s u", g=2, t=4, u=2)
-
-        def turn_values(g, u, copy):
-            bank = psum_y.tile([P, 4 * P], F32, name="bank")
-            for t in range(4):
-                nc.tensor.transpose(bank[:, t * P : (t + 1) * P], pairs[:, g, t, :, u], ident[:])
+        def round_tokens(copy, u, first, begin, end):
+            tokens = windows[u][:].rearrange("p (n e) -> p n e", e=2)
             copy(
-                vq[:, g, :].rearrange("s (r u e t) -> s r u e t", u=2, e=2, t=4)[:, :, u],
-                bank[:].bitcast(BF16).rearrange("s (t r e) -> s r e t", t=4, e=2),
+                tokens[:, first + begin : first + end, :],
+                chunks[(u, first)][:, :, begin:end].rearrange("p e n -> p n e"),
             )
 
-        def quantize_keys(g):
-            half = slice(g * 512, (g + 1) * 512)
-            quantize(k_codes[:, half], k_scales[:, half], kq[:, g * 2048 : (g + 1) * 2048])
+        def scalar_copy(dst, src):
+            nc.scalar.activation(dst, src, COPY)
 
-        def quantize_values(g):
-            quantize(v_codes[:, g, :], v_scales[:, g, :], vq[:, g, :])
+        def gather_latents(u, g):
+            words = grouped[:].bitcast(U32).rearrange("p (g t s u) -> p g t s u", g=2, t=PLACES, u=2)
+            half_list = offsets[:, g * HALF // 16 : (g + 1) * HALF // 16]
+            nc.vector.tensor_copy(
+                words[:, g, :, :, u].rearrange("p t s -> p s t"), windows[u][:].bitcast(U32).indirect(half_list)
+            )
 
-        def scores(g, h):
-            bank = psum_y.tile([P, 4, P], F32, name="bank")
+        def gather_row(row, table):
+            nc.vector.tensor_copy(row[:], table[:].indirect(offsets[:]))
+
+        kb_columns = keep.tile([P, 2 * PLACES], F32, name="kb_columns")
+        ts_columns = keep.tile([P, 2 * PLACES], F32, name="ts_columns")
+
+        def turn_row(columns, row, g):
+            bank = other_banks.tile([P, PLACES, P], F32, name="bank")
+            places = row[:, g * HALF : (g + 1) * HALF].rearrange("p (s t) -> p t s", t=PLACES)
+            for t in range(PLACES):
+                nc.tensor.transpose(bank[:, t, :], places[:, t, :], identity[:])
+            nc.scalar.activation(columns[:, PLACES * g : PLACES * (g + 1)], bank[:, :, 0], COPY)
+
+        def quantise(codes, scales, values):
+            nc.vector.quantize_mx(out=codes.bitcast(FP8X4), scales=scales, in_=values)
+
+        key_codes = keep.tile([P, N], U32, name="key_codes", align_bytes=64)
+        key_scales = keep.tile([P, N], U8, name="key_scales", align_bytes=64)
+        q_codes = keep.tile([P, NQ], U32, name="q_codes", align_bytes=64)
+        q_scales = keep.tile([P, NQ], U8, name="q_scales", align_bytes=64)
+        q_grouped = keep.tile([P, NQ * PLACES], BF16, name="q_grouped", align_bytes=64)
+        value_codes = keep.tile([P, 2, D], U32, name="value_codes", align_bytes=64)
+        value_scales = keep.tile([P, 2, D], U8, name="value_scales", align_bytes=64)
+        value_grouped = keep.tile([P, 2, D * PLACES], BF16, name="value_grouped", align_bytes=64)
+        weight_codes = keep.tile([P, 2, 2, P], U32, name="weight_codes", align_bytes=64)
+        weight_scales = keep.tile([P, 2, 2, P], U8, name="weight_scales", align_bytes=64)
+        weight_grouped = keep.tile([P, 2, 2, P * PLACES], BF16, name="weight_grouped", align_bytes=64)
+
+        def round_queries():
+            scalar_copy(q_grouped[:].rearrange("p (q f) -> p q f", f=PLACES), q_raw[:].rearrange("p f q -> p q f"))
+
+        def quantise_queries():
+            quantise(q_codes[:], q_scales[:], q_grouped[:])
+
+        def quantise_keys(g):
+            slots = slice(g * HALF, (g + 1) * HALF)
+            quantise(key_codes[:, slots], key_scales[:, slots], grouped[:, g * HALF * PLACES : (g + 1) * HALF * PLACES])
+
+        def turn_values(copy, g, u):
+            words = grouped[:].bitcast(F32).rearrange("p (g t s u) -> p g t s u", g=2, t=PLACES, u=2)
+            bank = other_banks.tile([P, PLACES * P], F32, name="bank")
+            for t in range(PLACES):
+                nc.tensor.transpose(bank[:, t * P : (t + 1) * P], words[:, g, t, :, u], identity[:])
+            copy(
+                value_grouped[:, g, :].rearrange("s (p u e t) -> s p u e t", u=2, e=2, t=PLACES)[:, :, u],
+                bank[:].bitcast(BF16).rearrange("s (t p e) -> s p e t", t=PLACES, e=2),
+            )
+
+        def quantise_values(g):
+            quantise(value_codes[:, g, :], value_scales[:, g, :], value_grouped[:, g, :])
+
+        scaled = keep.tile([P, 2 * PLACES, NQ], F32, name="scaled")
+        score_bank = {}
+        turned_scores = {}
+
+        def score(g, h):
+            bank = score_banks.tile([P, PLACES, P], F32, name="bank")
             queries = slice(h * P, (h + 1) * P)
-            for t in range(4):
-                cols = slice((4 * g + t) * P, (4 * g + t + 1) * P)
+            for t in range(PLACES):
+                slots = slice((PLACES * g + t) * P, (PLACES * g + t + 1) * P)
                 nc.tensor.matmul_mx(
                     out=bank[:, t, :],
-                    lhsT=k_codes[:, cols].bitcast(FP8X4),
-                    lhsT_scale=k_scales[:, cols],
+                    lhsT=key_codes[:, slots].bitcast(FP8X4),
+                    lhsT_scale=key_scales[:, slots],
                     rhs=q_codes[:, queries].bitcast(FP8X4),
                     rhs_scale=q_scales[:, queries],
                     start=True,
                     stop=True,
                 )
-            return bank
+            score_bank[(g, h)] = bank
 
-        def scale_scores(g, h, bank, engine):
-            for t in range(4):
-                b = 4 * g + t
-                dst = y[:, b, h * P : (h + 1) * P]
-                if engine == "scalar":
-                    nc.scalar.activation(
-                        dst, bank[:, t, :], IDENTITY, bias=kb_cols[:, b : b + 1], scale=ts_cols[:, b : b + 1]
-                    )
-                else:
-                    nc.vector.tensor_scalar(
-                        dst, bank[:, t, :], ts_cols[:, b : b + 1], kb_cols[:, b : b + 1], MULT, ADD
-                    )
+        def scale_scores(g, h):
+            for t in range(PLACES):
+                i = PLACES * g + t
+                nc.scalar.activation(
+                    scaled[:, i, h * P : (h + 1) * P],
+                    score_bank[(g, h)][:, t, :],
+                    IDENTITY,
+                    bias=kb_columns[:, i : i + 1],
+                    scale=ts_columns[:, i : i + 1],
+                )
 
         def turn_scores(g, h):
-            bank = psum_y.tile([P, 4 * P], F32, name="bank")
-            for t in range(4):
-                nc.tensor.transpose(bank[:, t * P : (t + 1) * P], y[:, 4 * g + t, h * P : (h + 1) * P], ident[:])
-            y_t[(h, g)] = bank
+            bank = other_banks.tile([P, PLACES * P], F32, name="bank")
+            for t in range(PLACES):
+                nc.tensor.transpose(
+                    bank[:, t * P : (t + 1) * P], scaled[:, PLACES * g + t, h * P : (h + 1) * P], identity[:]
+                )
+            turned_scores[(g, h)] = bank
 
         maxima = keep.tile([P, 4], F32, name="maxima")
-        neg_max = keep.tile([P, 2], F32, name="neg_max")
-        sums = keep.tile([P, 4], F32, name="sums")
-        total = keep.tile([P, 2], F32, name="total")
-        inv = keep.tile([P, 2], F32, name="inv")
-        p = keep.tile([P, 2, N], F32, name="p")
+        minus_max = keep.tile([P, 2], F32, name="minus_max")
+        part_sums = keep.tile([P, 4], F32, name="part_sums")
+        row_sums = keep.tile([P, 2], F32, name="row_sums")
+        inverse = keep.tile([P, 2], F32, name="inverse")
+        exponentials = keep.tile([P, 2, N], F32, name="exponentials")
 
-        def maximum(h, g):
-            i = 2 * h + g
-            nc.vector.reduce_max(maxima[:, i : i + 1], y_t[(h, g)][:], axis=X)
+        def find_maximum(g, h):
+            nc.vector.reduce_max(maxima[:, 2 * h + g : 2 * h + g + 1], turned_scores[(g, h)][:], axis=X)
 
-        def negate_maximum(h):
-            nc.vector.tensor_scalar(
-                neg_max[:, h : h + 1], maxima[:, 2 * h : 2 * h + 1], maxima[:, 2 * h + 1 : 2 * h + 2], -1.0, MAX, MULT
-            )
+        def join_maxima(h):
+            first, second = maxima[:, 2 * h : 2 * h + 1], maxima[:, 2 * h + 1 : 2 * h + 2]
+            nc.vector.tensor_scalar(minus_max[:, h : h + 1], first, second, -1.0, MAX, MULT)
 
-        def exponentials(h, g):
-            i = 2 * h + g
+        def exponentiate(g, h):
             nc.scalar.activation(
-                p[:, h, g * 512 : (g + 1) * 512],
-                y_t[(h, g)][:],
+                exponentials[:, h, g * HALF : (g + 1) * HALF],
+                turned_scores[(g, h)][:],
                 EXP,
-                bias=neg_max[:, h : h + 1],
-                accum_out=sums[:, i : i + 1],
+                bias=minus_max[:, h : h + 1],
+                accum_out=part_sums[:, 2 * h + g : 2 * h + g + 1],
             )
 
-        wq = keep.tile([P, 4, 512], BF16, name="wq", align_bytes=64)
-        w_codes = keep.tile([P, 4, P], U32, name="w_codes", align_bytes=64)
-        w_scales = keep.tile([P, 4, P], U8, name="w_scales", align_bytes=64)
-
-        p_t = {}
-
-        def turn_exponentials(h, g):
-            bank = psum_y.tile([P, 4, P], F32, name="bank")
-            for t in range(4):
-                nc.tensor.transpose(bank[:, t, :], p[:, h, g * 512 + t * P : g * 512 + (t + 1) * P], ident[:])
-            p_t[(h, g)] = bank
-
-        def weights(h, g):
-            i = 2 * h + g
+        def invert_row_sum(h):
             nc.vector.tensor_tensor(
-                wq[:, i, :].rearrange("s (q t) -> s q t", t=4),
-                p_t[(h, g)][:].rearrange("s t q -> s q t"),
-                ts_cols[:, 4 * g : 4 * g + 4].unsqueeze(1).to_broadcast([P, P, 4]),
+                row_sums[:, h : h + 1], part_sums[:, 2 * h : 2 * h + 1], part_sums[:, 2 * h + 1 : 2 * h + 2], ADD
+            )
+            nc.vector.reciprocal(inverse[:, h : h + 1], row_sums[:, h : h + 1])
+
+        turned_exponentials = {}
+
+        def turn_exponentials(g, h):
+            bank = score_banks.tile([P, PLACES, P], F32, name="bank")
+            for t in range(PLACES):
+                first = g * HALF + t * P
+                nc.tensor.transpose(bank[:, t, :], exponentials[:, h, first : first + P], identity[:])
+            turned_exponentials[(g, h)] = bank
+
+        def weigh(g, h):
+            nc.vector.tensor_tensor(
+                weight_grouped[:, h, g, :].rearrange("s (r t) -> s r t", t=PLACES),
+                turned_exponentials[(g, h)][:].rearrange("s t r -> s r t"),
+                ts_columns[:, PLACES * g : PLACES * (g + 1)].unsqueeze(1).to_broadcast([P, P, PLACES]),
                 MULT,
             )
 
-        def quantize_weights(h, g):
-            i = 2 * h + g
-            quantize(w_codes[:, i, :], w_scales[:, i, :], wq[:, i, :])
+        def quantise_weights(g, h):
+            quantise(weight_codes[:, h, g, :], weight_scales[:, h, g, :], weight_grouped[:, h, g, :])
 
-        def product(h):
-            acc = psum_s.tile([P, D], F32, name="bank")
+        output_bank = {}
+
+        def multiply_values(h):
+            bank = other_banks.tile([P, D], F32, name="bank")
             for g in range(2):
-                i = 2 * h + g
                 nc.tensor.matmul_mx(
-                    out=acc[:],
-                    lhsT=w_codes[:, i, :].bitcast(FP8X4),
-                    lhsT_scale=w_scales[:, i, :],
-                    rhs=v_codes[:, g, :].bitcast(FP8X4),
-                    rhs_scale=v_scales[:, g, :],
+                    out=bank[:],
+                    lhsT=weight_codes[:, h, g, :].bitcast(FP8X4),
+                    lhsT_scale=weight_scales[:, h, g, :],
+                    rhs=value_codes[:, g, :].bitcast(FP8X4),
+                    rhs_scale=value_scales[:, g, :],
                     start=(g == 0),
                     stop=(g == 1),
                 )
-            return acc
+            output_bank[h] = bank
 
-        def finish(h, acc, width):
+        def store_output(h, pieces):
             result = keep.tile([P, D], F32, name=f"result{h}")
-            for e in range(0, D, width):
-                part = slice(e, e + width)
+            width = D // pieces
+            for first in range(0, D, width):
+                cols = slice(first, first + width)
                 nc.vector.scalar_tensor_tensor(
-                    result[:, part], acc[:, part], inv[:, h : h + 1], ch_sb[:, part], MULT, MULT
+                    result[:, cols], output_bank[h][:, cols], inverse[:, h : h + 1], ch_tile[:, cols], MULT, MULT
                 )
-                nc.sync.dma_start(out=out[0, h * P : (h + 1) * P, part], in_=result[:, part])
+                nc.sync.dma_start(out=out[0, h * P : (h + 1) * P, cols], in_=result[:, cols])
 
-        def divide(h):
-            nc.vector.tensor_tensor(
-                total[:, h : h + 1], sums[:, 2 * h : 2 * h + 1], sums[:, 2 * h + 1 : 2 * h + 2], ADD
-            )
-            nc.vector.reciprocal(inv[:, h : h + 1], total[:, h : h + 1])
+        round_tokens(nc.vector.tensor_copy, 0, 1024, 0, 768)
+        round_tokens(scalar_copy, 0, 1024, 768, 1024)
+        round_tokens(nc.vector.tensor_copy, 0, 0, 0, 1024)
+        round_queries()
+        gather_row(ts_row, ts_table)
+        round_tokens(nc.vector.tensor_copy, 1, 1024, 0, 128)
+        round_tokens(scalar_copy, 1, 1024, 128, 512)
+        gather_row(kb_row, kb_table)
+        gather_latents(0, 0)
+        round_tokens(nc.vector.tensor_copy, 1, 0, 0, 1024)
+        turn_values(nc.scalar.copy, 0, 0)
+        round_tokens(scalar_copy, 1, 1536, 0, 512)
+        gather_latents(1, 0)
+        gather_latents(0, 1)
+        turn_values(nc.scalar.copy, 1, 0)
+        quantise_queries()
+        quantise_keys(0)
+        gather_latents(1, 1)
+        quantise_keys(1)
+        turn_row(kb_columns, kb_row, 1)
+        turn_row(kb_columns, kb_row, 0)
+        turn_row(ts_columns, ts_row, 1)
+        turn_values(nc.scalar.copy, 0, 1)
+        quantise_values(0)
+        turn_row(ts_columns, ts_row, 0)
 
-        banks = {}
-        accs = {}
-        cast("scalar", 1, 1024, 0, 512)
-        cast("vector", 1, 0, 0, 1024)
-        cast("vector", 0, 0, 0, 1024)
-        cast("vector", 0, 1024, 0, 1024)
-        gather_pairs(0, 1)
-        kb_row = gather_row(kb_sb, "kb")
-        cast("vector", 1, 1536, 0, 128)
-        cast("scalar", 1, 1536, 128, 512)
-        nc.scalar.activation(q_grouped[:].rearrange("p (q t) -> p q t", t=4), q_raw[:].rearrange("p t q -> p q t"), COPY)
-        gather_pairs(1, 0)
-        columns(kb_row, kb_cols, psum_s, 1)
-        gather_pairs(0, 0)
-        gather_pairs(1, 1)
-        quantize_keys(0)
-        ts_row = gather_row(ts_sb, "ts")
-        columns(ts_row, ts_cols, psum_s, 1)
-        quantize(q_codes[:], q_scales[:], q_grouped[:])
-        turn_values(0, 1, nc.scalar.copy)
-        quantize_keys(1)
-        banks[(0, 0)] = scores(0, 0)
-        turn_values(0, 0, nc.scalar.copy)
-        columns(ts_row, ts_cols, psum_s, 0)
-        columns(kb_row, kb_cols, psum_s, 0)
-        banks[(1, 0)] = scores(1, 0)
-        banks[(1, 1)] = scores(1, 1)
-        turn_values(1, 0, nc.scalar.copy)
-        turn_values(1, 1, nc.vector.tensor_copy)
-        quantize_values(0)
-        banks[(0, 1)] = scores(0, 1)
-        scale_scores(0, 0, banks[(0, 0)], "scalar")
-        scale_scores(1, 0, banks[(1, 0)], "scalar")
-        turn_scores(1, 0)
-        maximum(0, 1)
-        scale_scores(0, 1, banks[(0, 1)], "scalar")
-        quantize_values(1)
+        score(1, 0)
+        score(0, 0)
+        score(0, 1)
+        turn_values(nc.vector.tensor_copy, 1, 1)
+        scale_scores(0, 0)
+        scale_scores(1, 0)
         turn_scores(0, 0)
-        maximum(0, 0)
-        scale_scores(1, 1, banks[(1, 1)], "scalar")
-        turn_scores(0, 1)
-        negate_maximum(0)
+        find_maximum(0, 0)
+        score(1, 1)
+        quantise_values(1)
+        turn_scores(1, 0)
+        find_maximum(1, 0)
+        join_maxima(0)
+        exponentiate(0, 0)
+        scale_scores(1, 1)
         turn_scores(1, 1)
-        exponentials(0, 0)
-        maximum(1, 1)
+        scale_scores(0, 1)
+        turn_scores(0, 1)
+        for g in range(2):
+            find_maximum(g, 1)
+        exponentiate(1, 0)
         turn_exponentials(0, 0)
-        maximum(1, 0)
-        negate_maximum(1)
-        exponentials(1, 0)
-        exponentials(1, 1)
+        join_maxima(1)
         turn_exponentials(1, 0)
-        exponentials(0, 1)
+        exponentiate(0, 1)
         turn_exponentials(0, 1)
-        divide(0)
+        weigh(0, 1)
+        quantise_weights(0, 1)
+        weigh(1, 0)
+        quantise_weights(1, 0)
+        weigh(0, 0)
+        invert_row_sum(0)
+        exponentiate(1, 1)
         turn_exponentials(1, 1)
-        weights(1, 0)
-        weights(0, 0)
-        quantize_weights(0, 0)
-        weights(0, 1)
-        quantize_weights(1, 0)
-        quantize_weights(0, 1)
-        weights(1, 1)
-        quantize_weights(1, 1)
-        divide(1)
-        accs[0] = product(0)
-        finish(0, accs[0], D // 1)
-        accs[1] = product(1)
-        finish(1, accs[1], D // 2)
+        quantise_weights(0, 0)
+        invert_row_sum(1)
+        weigh(1, 1)
+        multiply_values(0)
+        quantise_weights(1, 1)
+        store_output(0, pieces=1)
+        multiply_values(1)
+        store_output(1, pieces=2)

from contextlib import ExitStack

import concourse.mybir as mybir
from concourse.masks import make_identity

F32 = mybir.dt.float32
BF16 = mybir.dt.bfloat16
U32 = mybir.dt.uint32
U16 = mybir.dt.uint16
U8 = mybir.dt.uint8
FP8X4 = mybir.dt.float8_e4m3fn_x4
ADD = mybir.AluOpType.add
MULT = mybir.AluOpType.mult
MAX = mybir.AluOpType.max
X = mybir.AxisListType.X
COPY = mybir.ActivationFunctionType.Copy
IDENTITY = mybir.ActivationFunctionType.Identity
EXP = mybir.ActivationFunctionType.Exp

P = 128
D = 512
T = 2048
N = 1024
NQ = 256
HALF = N // 2
PLACES = 4

FLOPS = 2 * (2 * NQ * N * D)
BYTES = 4 * (D * NQ + D * N + 2 * N + D + NQ * D) + 2 * N


def tile_attend_x_mla_bias_topk_kernel(tc, qT, cT, ts, kb, ch, offs, out):
    nc = tc.nc
    with ExitStack() as ctx:
        keep = ctx.enter_context(tc.tile_pool(name="keep", bufs=1))
        score_banks = ctx.enter_context(tc.psum_pool(name="score_banks", bufs=3))
        other_banks = ctx.enter_context(tc.psum_pool(name="other_banks", bufs=5))

        offsets = keep.tile([P, N // 16], U16, name="offsets")
        nc.sync.dma_start(offsets[:], offs)

        latent_rows = cT.rearrange("(p f) c -> p f c", f=PLACES)
        chunks = {}

        def load_chunk(u, first, width):
            chunk = keep.tile([P, 2, width], F32, name=f"chunk_{u}_{first}")
            nc.sync.dma_start(
                out=chunk[:], in_=latent_rows[:, 2 * u : 2 * u + 2, first : first + width]
            )
            chunks[(u, first)] = chunk

        def load_table(table, name):
            tile = keep.tile([P, T], F32, name=f"{name}_table")
            nc.sync.dma_start(out=tile[:], in_=table)
            return tile

        load_chunk(0, 0, 1024)
        load_chunk(0, 1024, 1024)
        load_chunk(1, 1536, 512)
        kb_table = load_table(kb, "kb")
        ts_table = load_table(ts, "ts")
        load_chunk(1, 1024, 512)
        load_chunk(1, 0, 1024)
        q_raw = keep.tile([P, PLACES, NQ], F32, name="q_raw")
        nc.sync.dma_start(out=q_raw[:], in_=qT[0].rearrange("(p f) q -> p f q", f=PLACES))
        ch_tile = keep.tile([P, D], F32, name="ch_tile")
        nc.sync.dma_start(out=ch_tile[:], in_=ch)

        identity = keep.tile([P, P], F32, name="identity")
        make_identity(nc, identity[:])
        zero = keep.tile([P, 1], F32, name="zero")
        nc.vector.memset(zero[:], 0.0)
        one = keep.tile([P, 1], F32, name="one")
        nc.scalar.activation(one[:], zero[:], EXP)

        windows = [keep.tile([P, 2 * T], BF16, name=f"window{u}", align_bytes=64) for u in range(2)]
        grouped = keep.tile([P, N * PLACES], BF16, name="grouped", align_bytes=64)
        kb_row = keep.tile([P, N], F32, name="kb_row")
        ts_row = keep.tile([P, N], F32, name="ts_row")

        def round_tokens(copy, u, first, begin, end):
            tokens = windows[u][:].rearrange("p (n e) -> p n e", e=2)
            copy(
                tokens[:, first + begin : first + end, :],
                chunks[(u, first)][:, :, begin:end].rearrange("p e n -> p n e"),
            )

        def scalar_copy(dst, src):
            nc.scalar.activation(dst, src, COPY)

        def gather_latents(u, g):
            words = grouped[:].bitcast(U32).rearrange("p (g t s u) -> p g t s u", g=2, t=PLACES, u=2)
            half_list = offsets[:, g * HALF // 16 : (g + 1) * HALF // 16]
            nc.vector.tensor_copy(
                words[:, g, :, :, u].rearrange("p t s -> p s t"), windows[u][:].bitcast(U32).indirect(half_list)
            )

        def gather_row(row, table):
            nc.vector.tensor_copy(row[:], table[:].indirect(offsets[:]))

        kb_columns = keep.tile([P, 2 * PLACES], F32, name="kb_columns")
        ts_columns = keep.tile([P, 2 * PLACES], F32, name="ts_columns")

        def turn_row(columns, row, g):
            bank = other_banks.tile([P, PLACES, P], F32, name="bank")
            places = row[:, g * HALF : (g + 1) * HALF].rearrange("p (s t) -> p t s", t=PLACES)
            for t in range(PLACES):
                nc.tensor.transpose(bank[:, t, :], places[:, t, :], identity[:])
            nc.scalar.activation(columns[:, PLACES * g : PLACES * (g + 1)], bank[:, :, 0], COPY)

        def quantise(codes, scales, values):
            nc.vector.quantize_mx(out=codes.bitcast(FP8X4), scales=scales, in_=values)

        key_codes = keep.tile([P, N], U32, name="key_codes", align_bytes=64)
        key_scales = keep.tile([P, N], U8, name="key_scales", align_bytes=64)
        q_codes = keep.tile([P, NQ], U32, name="q_codes", align_bytes=64)
        q_scales = keep.tile([P, NQ], U8, name="q_scales", align_bytes=64)
        q_grouped = keep.tile([P, NQ * PLACES], BF16, name="q_grouped", align_bytes=64)
        value_codes = keep.tile([P, 2, D], U32, name="value_codes", align_bytes=64)
        value_scales = keep.tile([P, 2, D], U8, name="value_scales", align_bytes=64)
        value_grouped = keep.tile([P, 2, D * PLACES], BF16, name="value_grouped", align_bytes=64)
        weight_codes = keep.tile([P, 2, 2, P], U32, name="weight_codes", align_bytes=64)
        weight_scales = keep.tile([P, 2, 2, P], U8, name="weight_scales", align_bytes=64)
        weight_grouped = keep.tile([P, 2, 2, P * PLACES], BF16, name="weight_grouped", align_bytes=64)

        def round_queries():
            scalar_copy(q_grouped[:].rearrange("p (q f) -> p q f", f=PLACES), q_raw[:].rearrange("p f q -> p q f"))

        def quantise_queries():
            quantise(q_codes[:], q_scales[:], q_grouped[:])

        def quantise_keys(g):
            slots = slice(g * HALF, (g + 1) * HALF)
            quantise(key_codes[:, slots], key_scales[:, slots], grouped[:, g * HALF * PLACES : (g + 1) * HALF * PLACES])

        def turn_values(copy, g, u):
            words = grouped[:].bitcast(F32).rearrange("p (g t s u) -> p g t s u", g=2, t=PLACES, u=2)
            bank = other_banks.tile([P, PLACES * P], F32, name="bank")
            for t in range(PLACES):
                nc.tensor.transpose(bank[:, t * P : (t + 1) * P], words[:, g, t, :, u], identity[:])
            copy(
                value_grouped[:, g, :].rearrange("s (p u e t) -> s p u e t", u=2, e=2, t=PLACES)[:, :, u],
                bank[:].bitcast(BF16).rearrange("s (t p e) -> s p e t", t=PLACES, e=2),
            )

        def quantise_values(g):
            quantise(value_codes[:, g, :], value_scales[:, g, :], value_grouped[:, g, :])

        scaled = keep.tile([P, 2 * PLACES, NQ], F32, name="scaled")
        score_bank = {}
        turned_scores = {}

        def score(g, h):
            bank = score_banks.tile([P, PLACES, P], F32, name="bank")
            queries = slice(h * P, (h + 1) * P)
            for t in range(PLACES):
                slots = slice((PLACES * g + t) * P, (PLACES * g + t + 1) * P)
                nc.tensor.matmul_mx(
                    out=bank[:, t, :],
                    lhsT=key_codes[:, slots].bitcast(FP8X4),
                    lhsT_scale=key_scales[:, slots],
                    rhs=q_codes[:, queries].bitcast(FP8X4),
                    rhs_scale=q_scales[:, queries],
                    start=True,
                    stop=True,
                )
            score_bank[(g, h)] = bank

        def scale_scores(g, h):
            for t in range(PLACES):
                i = PLACES * g + t
                nc.scalar.activation(
                    scaled[:, i, h * P : (h + 1) * P],
                    score_bank[(g, h)][:, t, :],
                    IDENTITY,
                    bias=kb_columns[:, i : i + 1],
                    scale=ts_columns[:, i : i + 1],
                )

        def turn_scores(g, h):
            bank = other_banks.tile([P, PLACES * P], F32, name="bank")
            for t in range(PLACES):
                nc.tensor.transpose(
                    bank[:, t * P : (t + 1) * P], scaled[:, PLACES * g + t, h * P : (h + 1) * P], identity[:]
                )
            turned_scores[(g, h)] = bank

        maxima = keep.tile([P, 4], F32, name="maxima")
        minus_max = keep.tile([P, 2], F32, name="minus_max")
        part_sums = keep.tile([P, 4], F32, name="part_sums")
        row_sums = keep.tile([P, 2], F32, name="row_sums")
        inverse = keep.tile([P, 2], F32, name="inverse")
        exponentials = keep.tile([P, 2, N], F32, name="exponentials")

        def find_maximum(g, h):
            nc.vector.reduce_max(maxima[:, 2 * h + g : 2 * h + g + 1], turned_scores[(g, h)][:], axis=X)

        def join_maxima(h):
            first, second = maxima[:, 2 * h : 2 * h + 1], maxima[:, 2 * h + 1 : 2 * h + 2]
            nc.vector.tensor_scalar(minus_max[:, h : h + 1], first, second, -1.0, MAX, MULT)

        def exponentiate(g, h):
            nc.scalar.activation(
                exponentials[:, h, g * HALF : (g + 1) * HALF],
                turned_scores[(g, h)][:],
                EXP,
                bias=minus_max[:, h : h + 1],
                accum_out=part_sums[:, 2 * h + g : 2 * h + g + 1],
            )

        def invert_row_sum(h):
            nc.vector.tensor_tensor(
                row_sums[:, h : h + 1], part_sums[:, 2 * h : 2 * h + 1], part_sums[:, 2 * h + 1 : 2 * h + 2], ADD
            )
            nc.vector.reciprocal(inverse[:, h : h + 1], row_sums[:, h : h + 1])

        turned_exponentials = {}

        def turn_exponentials(g, h):
            bank = score_banks.tile([P, PLACES, P], F32, name="bank")
            for t in range(PLACES):
                first = g * HALF + t * P
                nc.tensor.transpose(bank[:, t, :], exponentials[:, h, first : first + P], identity[:])
            turned_exponentials[(g, h)] = bank

        def weigh(g, h):
            nc.vector.tensor_tensor(
                weight_grouped[:, h, g, :].rearrange("s (r t) -> s r t", t=PLACES),
                turned_exponentials[(g, h)][:].rearrange("s t r -> s r t"),
                ts_columns[:, PLACES * g : PLACES * (g + 1)].unsqueeze(1).to_broadcast([P, P, PLACES]),
                MULT,
            )

        def quantise_weights(g, h):
            quantise(weight_codes[:, h, g, :], weight_scales[:, h, g, :], weight_grouped[:, h, g, :])

        output_bank = {}

        def multiply_values(h):
            bank = other_banks.tile([P, D], F32, name="bank")
            for g in range(2):
                nc.tensor.matmul_mx(
                    out=bank[:],
                    lhsT=weight_codes[:, h, g, :].bitcast(FP8X4),
                    lhsT_scale=weight_scales[:, h, g, :],
                    rhs=value_codes[:, g, :].bitcast(FP8X4),
                    rhs_scale=value_scales[:, g, :],
                    start=(g == 0),
                    stop=(g == 1),
                )
            output_bank[h] = bank

        def store_output(h, pieces):
            result = keep.tile([P, D], F32, name=f"result{h}")
            width = D // pieces
            for first in range(0, D, width):
                cols = slice(first, first + width)
                nc.vector.scalar_tensor_tensor(
                    result[:, cols], output_bank[h][:, cols], inverse[:, h : h + 1], ch_tile[:, cols], MULT, MULT
                )
                nc.sync.dma_start(out=out[0, h * P : (h + 1) * P, cols], in_=result[:, cols])

        round_tokens(nc.vector.tensor_copy, 0, 1024, 0, 768)
        round_tokens(scalar_copy, 0, 1024, 768, 1024)
        round_tokens(nc.vector.tensor_copy, 0, 0, 0, 1024)
        round_queries()
        gather_row(ts_row, ts_table)
        round_tokens(nc.vector.tensor_copy, 1, 1024, 0, 128)
        round_tokens(scalar_copy, 1, 1024, 128, 512)
        gather_row(kb_row, kb_table)
        gather_latents(0, 0)
        round_tokens(nc.vector.tensor_copy, 1, 0, 0, 1024)
        turn_values(nc.scalar.copy, 0, 0)
        round_tokens(scalar_copy, 1, 1536, 0, 512)
        gather_latents(1, 0)
        gather_latents(0, 1)
        turn_values(nc.scalar.copy, 1, 0)
        quantise_queries()
        quantise_keys(0)
        gather_latents(1, 1)
        quantise_keys(1)
        turn_row(kb_columns, kb_row, 1)
        turn_row(kb_columns, kb_row, 0)
        turn_row(ts_columns, ts_row, 1)
        turn_values(nc.scalar.copy, 0, 1)
        quantise_values(0)
        turn_row(ts_columns, ts_row, 0)

        score(1, 0)
        score(0, 0)
        score(0, 1)
        turn_values(nc.vector.tensor_copy, 1, 1)
        scale_scores(0, 0)
        scale_scores(1, 0)
        turn_scores(0, 0)
        find_maximum(0, 0)
        score(1, 1)
        quantise_values(1)
        turn_scores(1, 0)
        find_maximum(1, 0)
        join_maxima(0)
        exponentiate(0, 0)
        scale_scores(1, 1)
        turn_scores(1, 1)
        scale_scores(0, 1)
        turn_scores(0, 1)
        for g in range(2):
            find_maximum(g, 1)
        exponentiate(1, 0)
        turn_exponentials(0, 0)
        join_maxima(1)
        turn_exponentials(1, 0)
        exponentiate(0, 1)
        turn_exponentials(0, 1)
        weigh(0, 1)
        quantise_weights(0, 1)
        weigh(1, 0)
        quantise_weights(1, 0)
        weigh(0, 0)
        invert_row_sum(0)
        exponentiate(1, 1)
        turn_exponentials(1, 1)
        quantise_weights(0, 0)
        invert_row_sum(1)
        weigh(1, 1)
        multiply_values(0)
        quantise_weights(1, 1)
        store_output(0, pieces=1)
        multiply_values(1)
        store_output(1, pieces=2)
